import numpy as np
import ml_dtypes


def mxq(x, axis, fmt="e4m3"):
    dtype, down = {"e4m3": (ml_dtypes.float8_e4m3fn, 7), "e5m2": (ml_dtypes.float8_e5m2, 14)}[fmt]
    v = np.moveaxis(np.asarray(x, np.float32).astype(ml_dtypes.bfloat16).astype(np.float64), axis, -1)
    blocks = v.reshape(v.shape[:-1] + (-1, 32))
    amax = np.abs(blocks).max(-1, keepdims=True)
    byte = np.maximum(np.where(amax > 0, np.frexp(amax)[1] - 1 + 127, 0) - down, 1)
    scale = np.exp2(byte - 127.0)
    codes = (blocks / scale).astype(np.float32).astype(dtype).astype(np.float64)
    return np.moveaxis((codes * scale).reshape(v.shape), -1, axis)


WIDE = False


def mx_kscale(k):
    if not WIDE:
        return np.ones(k)
    levels = np.array([30, -30])
    if k % 512:
        return np.exp2(np.random.permutation(np.resize(levels, k // 32))).repeat(32)
    a = np.empty((k // 512, 16))
    for p in range(k // 512):
        a[p, :8] = np.random.permutation(np.resize(levels, 8))
        for g in range(8):
            far = levels[np.abs(levels - a[p, g]) >= 10]
            a[p, g + 8] = far[np.random.randint(len(far))]
    return np.exp2(a.ravel()).repeat(32)


BF16 = ml_dtypes.bfloat16


def bf(x):
    return np.asarray(x, np.float32).astype(BF16)


def f64(x):
    return np.asarray(x).astype(np.float64)


E2M1 = np.array([0.0, 0.5, 1.0, 1.5, 2.0, 3.0, 4.0, 6.0, -0.0, -0.5, -1.0, -1.5, -2.0, -3.0, -4.0, -6.0])


def pack_weight(w, fmt):
    k, n = w.shape
    w = f64(bf(w)).reshape(k // 32, 32, n)
    amax = np.abs(w).max(1)
    if fmt in ("e4m3", "e5m2"):
        byte = np.frexp(amax)[1] - 1 + 127 - (7 if fmt == "e4m3" else 14)
    else:
        mant, ex = np.frexp(amax / 6.0)
        byte = np.where(mant > 0.5, ex, ex - 1) + 127
    byte = np.clip(np.where(amax > 0, byte, 1), 1, 254)
    scaled = (w * np.exp2(127.0 - byte)[:, None, :]).reshape(k, n).astype(np.float32)
    by_word = np.ascontiguousarray(scaled.reshape(k // 512, 128, 4, n).transpose(0, 1, 3, 2))
    if fmt in ("e4m3", "e5m2"):
        words = by_word.astype(ml_dtypes.float8_e4m3fn if fmt == "e4m3" else ml_dtypes.float8_e5m2).view(np.uint8)
    else:
        c = by_word.astype(ml_dtypes.float4_e2m1fn).view(np.uint8) & 0xF
        words = c[..., 0::2] | (c[..., 1::2] << 4)
    return np.ascontiguousarray(words), np.ascontiguousarray(byte.astype(np.uint8).reshape(k // 512, 16, n))


def unpack_weight(words, scales, fmt):
    g, p, n, _ = words.shape
    if fmt in ("e4m3", "e5m2"):
        vals = np.ascontiguousarray(words).view(ml_dtypes.float8_e4m3fn if fmt == "e4m3" else ml_dtypes.float8_e5m2).astype(np.float64)
    else:
        nib = np.empty((g, p, n, 4), np.uint8)
        nib[..., 0::2] = words & 0xF
        nib[..., 1::2] = words >> 4
        vals = E2M1[nib]
    vals = vals * np.repeat(np.exp2(scales.astype(np.float64) - 127.0), 8, axis=1)[..., None]
    return vals.transpose(0, 1, 3, 2).reshape(g * 512, n)


L, Y, F, J, O, C, E = 4, 2, 3, 512, 1024, 1024, 512
SLOPE = 0.125


def setup_inputs():
    s, t = mx_kscale(O), mx_kscale(C)
    y0, y1 = np.random.standard_t(6, (Y, O, J)) * s[:, None]
    G = np.stack([y0, y0 + y1, y0 - y1, -y1], axis=1).reshape(O, L * J)
    g_words, g_scales = pack_weight(G, "e5m2")
    f0, f1, f2 = np.random.standard_normal((F, C, O)) / np.sqrt(O) / s * t[:, None]
    u = np.stack([f0, (f0 + f1 + f2) / 2, (f0 - f1 + f2) / 2, f2])
    d = np.where(np.random.standard_normal((L, J, C)) > 0, 1.0, SLOPE)
    return {"g_words": g_words, "g_scales": g_scales,
            "u": bf(u),
            "d": bf(d),
            "w": bf(np.random.standard_normal((E, C)) / np.sqrt(C) / t)}


def reference(g_words, g_scales, u, d, w):
    gm = unpack_weight(g_words, g_scales, "e5m2")
    gm = gm.reshape(O, L, J).transpose(1, 2, 0)
    uq = mxq(f64(u), 2, "e4m3").swapaxes(1, 2)
    dv = gm @ uq
    dz = dv * f64(d)
    wq = mxq(f64(w), 1, "e4m3").T
    return mxq(dz, 2, "e5m2") @ wq

@@ -1,0 +1,272 @@
+from contextlib import ExitStack
+
+import concourse.mybir as mybir
+from concourse.masks import make_identity
+
+F32 = mybir.dt.float32
+BF16 = mybir.dt.bfloat16
+U32 = mybir.dt.uint32
+I32 = mybir.dt.int32
+U8 = mybir.dt.uint8
+E4 = mybir.dt.float8_e4m3fn_x4
+E5 = mybir.dt.float8_e5m2_x4
+
+L, J, O, C, E = 4, 512, 1024, 1024, 512
+FLOPS = 2 * L * J * C * (O + E)
+
+
+def tile_winograd_domain_backward_e3_kernel(tc, g_words, g_scales, u, d, w, out):
+    nc = tc.nc
+    with ExitStack() as ctx:
+        keep = ctx.enter_context(tc.tile_pool(name="keep", bufs=1))
+        work = ctx.enter_context(tc.tile_pool(name="work", bufs=2))
+        psum = ctx.enter_context(tc.psum_pool(name="psum", bufs=2))
+        ctx.enter_context(tc.manual_schedule())
+
+        ident = keep.tile([128, 128], F32, name="ident")
+        g_codes = keep.tile([128, 2, 2048], U32, name="g_codes", align_bytes=64)
+        g_sc = keep.tile([128, 2, 2048], U8, name="g_sc", align_bytes=64)
+        w_sb = keep.tile([128, 4, 1024], BF16, name="w_sb", align_bytes=64)
+        u_sb = {}
+        d_sb = {}
+        for l in range(L):
+            for h in range(2):
+                u_sb[l, h] = keep.tile([128, 4, 1024], BF16, name=f"u_sb_{l}_{h}", align_bytes=64)
+            d_sb[l] = keep.tile([128, 4, 1024], BF16, name=f"d_sb_{l}", align_bytes=64)
+
+        nc.vector.memset(g_sc[:].rearrange("p g n -> p (g n)").bitcast(I32), 0)
+        make_identity(nc, ident[:])
+
+        def load_u(l, h, pieces):
+            rows = u[l, 512 * h : 512 * h + 512, :].rearrange("(p c) o -> p c o", c=4)
+            n = 4 // pieces
+            for i in range(pieces):
+                nc.sync.dma_start(out=u_sb[l, h][:, n * i : n * i + n, :], in_=rows[:, n * i : n * i + n, :])
+
+        def load_d(l, j0, j1):
+            rows = d[l].rearrange("(b p) c -> p b c", p=128)
+            nc.sync.dma_start(out=d_sb[l][:, j0:j1, :], in_=rows[:, j0:j1, :])
+
+        def load_g(l0, l1):
+            rows = g_words.rearrange("g p n t -> p g (n t)")
+            nc.sync.dma_start(out=g_codes[:, :, 512 * l0 : 512 * l1].bitcast(I32),
+                              in_=rows[:, :, 2048 * l0 : 2048 * l1].bitcast(I32))
+
+        load_u(0, 0, 2)
+        load_g(0, 1)
+        load_d(0, 0, 2)
+        load_u(0, 1, 2)
+        load_d(0, 2, 4)
+        nc.sync.dma_start(out=w_sb[:], in_=w.rearrange("(b p) c -> p b c", p=128))
+        load_u(1, 0, 1)
+        load_u(1, 1, 1)
+        load_g(1, 2)
+        load_d(1, 0, 2)
+        load_d(1, 2, 4)
+        load_u(2, 0, 1)
+        load_u(2, 1, 1)
+        load_g(2, 4)
+        load_d(2, 0, 4)
+        load_u(3, 0, 1)
+        load_u(3, 1, 1)
+        load_d(3, 0, 4)
+        sc_rows = g_scales.bitcast(I32).rearrange("g (q r) n -> r q g n", r=4)
+        for r in range(4):
+            nc.scalar.dma_start(out=g_sc[r:128:32, :, :].bitcast(I32), in_=sc_rows[r])
+
+        def copy(engine, dst, src):
+            if engine == "s":
+                nc.scalar.copy(dst, src)
+            else:
+                nc.vector.tensor_copy(out=dst, in_=src)
+
+        grouped = {}
+        perm = {}
+        quant = {}
+
+        def permute(key, src, g):
+            pt = work.tile([128, 4, 2, 128], F32, name="pt", bufs=3)
+            nc.vector.tensor_copy(
+                out=pt[:],
+                in_=src[:].bitcast(F32)[:, :, 256 * g : 256 * g + 256].rearrange("p c (k u) -> p c u k", u=2),
+            )
+            perm[key] = pt
+
+        def turn(key, src, g, cp, engine):
+            if cp == 0:
+                gt = work.tile([128, 2048], BF16, name="gt", bufs=4, align_bytes=64)
+                grouped[key] = gt
+            xt = psum.tile([128, 2, 2, 128], F32, name="xt", bufs=3)
+            for a in range(2):
+                for uu in range(2):
+                    if key in perm:
+                        words = perm[key][:, 2 * cp + a, uu, :]
+                    else:
+                        words = src[:].bitcast(F32)[:, 2 * cp + a, 256 * g + uu : 256 * g + 256 : 2]
+                    nc.tensor.transpose(xt[:, a, uu, :], words, ident[:])
+            copy(engine,
+                 grouped[key][:].bitcast(F32)[:, 512 * cp : 512 * cp + 512].rearrange("p (a r u) -> p a r u", a=2, u=2),
+                 xt[:].rearrange("p a u r -> p a r u"))
+
+        def quantise(key, pool, bufs, tag):
+            codes = pool.tile([128, 512], U32, name=tag + "_codes", bufs=bufs, align_bytes=64)
+            sc = pool.tile([128, 512], U8, name=tag + "_sc", bufs=bufs, align_bytes=64)
+            nc.vector.quantize_mx(out=codes[:].bitcast(E4), scales=sc[:], in_=grouped[key][:])
+            quant[key] = (codes, sc)
+
+        def u_turn(l, q, engines="ss"):
+            h, g = q // 2, q % 2
+            for cp in range(2):
+                turn((l, q), u_sb[l, h], g, cp, engines[cp])
+
+        def u_perm(l, q):
+            permute((l, q), u_sb[l, q // 2], q % 2)
+
+        def u_quant(l, q):
+            quantise((l, q), work, 8, "uq")
+
+        dz = {}
+        acc1 = {}
+
+        def m1(l, jb, h):
+            acc = psum.tile([128, 512], F32, name="acc", bufs=3)
+            cols = slice(512 * l + 128 * jb, 512 * l + 128 * jb + 128)
+            for g in range(2):
+                codes, sc = quant[l, 2 * h + g]
+                nc.tensor.matmul_mx(
+                    out=acc[:],
+                    lhsT=g_codes[:, g, cols].bitcast(E5), lhsT_scale=g_sc[:, g, cols],
+                    rhs=codes[:].bitcast(E4), rhs_scale=sc[:],
+                    start=(g == 0), stop=(g == 1),
+                )
+            acc1[l, jb, h] = acc
+
+        def mult(l, jb, h):
+            if h == 0:
+                z = work.tile([128, 1024], BF16, name="z", bufs=6, align_bytes=64)
+                dz[l, jb] = z
+            half = slice(512 * h, 512 * h + 512)
+            nc.vector.tensor_tensor(
+                out=dz[l, jb][:, half].rearrange("j (u p e) -> j u p e", u=2, e=2),
+                in0=acc1[l, jb, h][:].rearrange("j (u e p) -> j u p e", u=2, e=2),
+                in1=d_sb[l][:, jb, half].rearrange("j (p u e) -> j u p e", u=2, e=2),
+                op=mybir.AluOpType.mult,
+            )
+
+        zg = {}
+        zq = {}
+
+        def z_turn(l, jb, engine="s"):
+            zt = work.tile([128, 1024], BF16, name="zt", bufs=4, align_bytes=64)
+            xt = psum.tile([128, 2, 2, 128], F32, name="xt", bufs=3)
+            words = dz[l, jb][:].bitcast(F32)
+            for h in range(2):
+                for uu in range(2):
+                    c0 = 256 * h + 128 * uu
+                    nc.tensor.transpose(xt[:, h, uu, :], words[:, c0 : c0 + 128], ident[:])
+            copy(engine,
+                 zt[:].bitcast(F32).rearrange("p (h j u) -> p h j u", h=2, u=2),
+                 xt[:].rearrange("p h u j -> p h j u"))
+            zg[l, jb] = zt
+
+        def z_quant(l, jb):
+            zc = work.tile([128, 256], U32, name="zc", bufs=6, align_bytes=64)
+            zs = work.tile([128, 256], U8, name="zs", bufs=6, align_bytes=64)
+            nc.vector.quantize_mx(out=zc[:].bitcast(E5), scales=zs[:], in_=zg[l, jb][:])
+            zq[l, jb] = (zc, zs)
+
+        def m2(l, jb, engine="s"):
+            acc = psum.tile([128, 512], F32, name="acc2", bufs=2)
+            zc, zs = zq[l, jb]
+            for h in range(2):
+                codes, sc = quant["w", h]
+                cols = slice(128 * h, 128 * h + 128)
+                nc.tensor.matmul_mx(
+                    out=acc[:],
+                    lhsT=zc[:, cols].bitcast(E5), lhsT_scale=zs[:, cols],
+                    rhs=codes[:].bitcast(E4), rhs_scale=sc[:],
+                    start=(h == 0), stop=(h == 1),
+                )
+            ot = work.tile([128, 512], F32, name="ot", bufs=6)
+            copy(engine, ot[:], acc[:])
+            nc.sync.dma_start(out=out[l, 128 * jb : 128 * jb + 128, :], in_=ot[:])
+
+        for q in (0, 2):
+            for cp in range(2):
+                turn((0, q), u_sb[0, q // 2], 0, cp, "s")
+                turn((0, q + 1), u_sb[0, q // 2], 1, cp, "v")
+            u_quant(0, q)
+            u_quant(0, q + 1)
+            if q == 0:
+                for jb in range(4):
+                    m1(0, jb, 0)
+                    mult(0, jb, 0)
+        for jb in range(2):
+            m1(0, jb, 1)
+            mult(0, jb, 1)
+        for g in range(2):
+            for cp in range(2):
+                turn(("w", g), w_sb, g, cp, "s")
+        z_turn(0, 0)
+        z_turn(0, 1)
+        u_perm(1, 0)
+        quantise(("w", 0), keep, 1, "wq0")
+        for jb in range(2, 4):
+            m1(0, jb, 1)
+            mult(0, jb, 1)
+        quantise(("w", 1), keep, 1, "wq1")
+        z_quant(0, 0)
+        z_quant(0, 1)
+        u_perm(1, 1)
+        u_turn(1, 0)
+        z_turn(0, 2)
+        z_turn(0, 3)
+        u_quant(1, 0)
+        u_perm(1, 2)
+        u_turn(1, 1)
+        u_turn(1, 2)
+        z_quant(0, 2)
+        z_quant(0, 3)
+        u_quant(1, 1)
+        u_perm(1, 3)
+
+        pending_u = (1, 2)
+        for l in range(1, L):
+            for i in range(4):
+                pair = [(0, 0), (1, 0)], [(2, 0), (3, 0)], [(0, 1), (1, 1)], [(2, 1), (3, 1)]
+                for jb, h in pair[i]:
+                    m1(l, jb, h)
+                    mult(l, jb, h)
+                if i == 0:
+                    m2(l - 1, 0)
+                    m2(l - 1, 1)
+                if i == 1:
+                    m2(l - 1, 2)
+                    m2(l - 1, 3)
+                now = (l, 3) if i == 0 else (l + 1, i - 1)
+                nxt = (l + 1, i)
+                if pending_u is not None:
+                    u_quant(*pending_u)
+                pending_u = None
+                if now[0] < L:
+                    u_turn(*now)
+                    pending_u = now
+                if i == 0 and l > 1:
+                    z_quant(l - 1, 2)
+                    z_quant(l - 1, 3)
+                if i == 2:
+                    z_turn(l, 0)
+                    z_turn(l, 1)
+                if i == 3:
+                    z_turn(l, 2)
+                    z_quant(l, 0)
+                    z_quant(l, 1)
+                    z_turn(l, 3)
+                if nxt[0] < L:
+                    u_perm(*nxt)
+        z_quant(3, 2)
+        m2(3, 0)
+        m2(3, 1)
+        z_quant(3, 3)
+        m2(3, 2)
+        m2(3, 3)

@@ -37,10 +37,10 @@ def tile_winograd_domain_backward_e3_kernel(tc, g_words, g_scales, u, d, w, out)
         nc.vector.memset(g_sc[:].rearrange("p g n -> p (g n)").bitcast(I32), 0)
         make_identity(nc, ident[:])
 
-        def load_u(l, h, pieces):
+        def load_u(l, h, pieces, which=None):
             rows = u[l, 512 * h : 512 * h + 512, :].rearrange("(p c) o -> p c o", c=4)
             n = 4 // pieces
-            for i in range(pieces):
+            for i in which or range(pieces):
                 nc.sync.dma_start(out=u_sb[l, h][:, n * i : n * i + n, :], in_=rows[:, n * i : n * i + n, :])
 
         def load_d(l, j0, j1):
@@ -53,9 +53,13 @@ def tile_winograd_domain_backward_e3_kernel(tc, g_words, g_scales, u, d, w, out)
                               in_=rows[:, :, 2048 * l0 : 2048 * l1].bitcast(I32))
 
         load_u(0, 0, 2)
+        sc_rows = g_scales.bitcast(I32).rearrange("g (q r) n -> r q g n", r=4)
+        for r in range(4):
+            nc.scalar.dma_start(out=g_sc[r:128:32, :, :].bitcast(I32), in_=sc_rows[r])
+        load_u(0, 1, 2, (0,))
         load_g(0, 1)
+        load_u(0, 1, 2, (1,))
         load_d(0, 0, 2)
-        load_u(0, 1, 2)
         load_d(0, 2, 4)
         nc.sync.dma_start(out=w_sb[:], in_=w.rearrange("(b p) c -> p b c", p=128))
         load_u(1, 0, 1)
@@ -70,9 +74,6 @@ def tile_winograd_domain_backward_e3_kernel(tc, g_words, g_scales, u, d, w, out)
         load_u(3, 0, 1)
         load_u(3, 1, 1)
         load_d(3, 0, 4)
-        sc_rows = g_scales.bitcast(I32).rearrange("g (q r) n -> r q g n", r=4)
-        for r in range(4):
-            nc.scalar.dma_start(out=g_sc[r:128:32, :, :].bitcast(I32), in_=sc_rows[r])
 
         def copy(engine, dst, src):
             if engine == "s":
@@ -96,7 +97,7 @@ def tile_winograd_domain_backward_e3_kernel(tc, g_words, g_scales, u, d, w, out)
             if cp == 0:
                 gt = work.tile([128, 2048], BF16, name="gt", bufs=4, align_bytes=64)
                 grouped[key] = gt
-            xt = psum.tile([128, 2, 2, 128], F32, name="xt", bufs=3)
+            xt = psum.tile([128, 2, 2, 128], F32, name="xt", bufs=4)
             for a in range(2):
                 for uu in range(2):
                     if key in perm:
@@ -129,7 +130,7 @@ def tile_winograd_domain_backward_e3_kernel(tc, g_words, g_scales, u, d, w, out)
         acc1 = {}
 
         def m1(l, jb, h):
-            acc = psum.tile([128, 512], F32, name="acc", bufs=3)
+            acc = psum.tile([128, 512], F32, name="acc", bufs=4)
             cols = slice(512 * l + 128 * jb, 512 * l + 128 * jb + 128)
             for g in range(2):
                 codes, sc = quant[l, 2 * h + g]
@@ -158,7 +159,7 @@ def tile_winograd_domain_backward_e3_kernel(tc, g_words, g_scales, u, d, w, out)
 
         def z_turn(l, jb, engine="s"):
             zt = work.tile([128, 1024], BF16, name="zt", bufs=4, align_bytes=64)
-            xt = psum.tile([128, 2, 2, 128], F32, name="xt", bufs=3)
+            xt = psum.tile([128, 2, 2, 128], F32, name="xt", bufs=4)
             words = dz[l, jb][:].bitcast(F32)
             for h in range(2):
                 for uu in range(2):
@@ -175,8 +176,8 @@ def tile_winograd_domain_backward_e3_kernel(tc, g_words, g_scales, u, d, w, out)
             nc.vector.quantize_mx(out=zc[:].bitcast(E5), scales=zs[:], in_=zg[l, jb][:])
             zq[l, jb] = (zc, zs)
 
-        def m2(l, jb, engine="s"):
-            acc = psum.tile([128, 512], F32, name="acc2", bufs=2)
+        def m2_acc(l, jb):
+            acc = psum.tile([128, 512], F32, name="acc", bufs=4)
             zc, zs = zq[l, jb]
             for h in range(2):
                 codes, sc = quant["w", h]
@@ -187,71 +188,79 @@ def tile_winograd_domain_backward_e3_kernel(tc, g_words, g_scales, u, d, w, out)
                     rhs=codes[:].bitcast(E4), rhs_scale=sc[:],
                     start=(h == 0), stop=(h == 1),
                 )
+            return acc
+
+        def m2(l, jb, engine="s"):
+            acc = m2_acc(l, jb)
             ot = work.tile([128, 512], F32, name="ot", bufs=6)
             copy(engine, ot[:], acc[:])
             nc.sync.dma_start(out=out[l, 128 * jb : 128 * jb + 128, :], in_=ot[:])
 
+        def m2_split(l, jb):
+            acc = m2_acc(l, jb)
+            for n, engine in enumerate("sv"):
+                half = slice(256 * n, 256 * n + 256)
+                oh = work.tile([128, 256], F32, name=f"oh{n}", bufs=1)
+                copy(engine, oh[:], acc[:, half])
+                nc.sync.dma_start(out=out[l, 128 * jb : 128 * jb + 128, half], in_=oh[:])
+
         for q in (0, 2):
             for cp in range(2):
                 turn((0, q), u_sb[0, q // 2], 0, cp, "s")
-                turn((0, q + 1), u_sb[0, q // 2], 1, cp, "v")
+                turn((0, q + 1), u_sb[0, q // 2], 1, cp, "v" if cp == 0 or q == 0 else "s")
             u_quant(0, q)
             u_quant(0, q + 1)
-            if q == 0:
-                for jb in range(4):
-                    m1(0, jb, 0)
-                    mult(0, jb, 0)
+        for jb in range(4):
+            m1(0, jb, 0)
+            mult(0, jb, 0)
         for jb in range(2):
             m1(0, jb, 1)
             mult(0, jb, 1)
-        for g in range(2):
-            for cp in range(2):
-                turn(("w", g), w_sb, g, cp, "s")
+        for cp in range(2):
+            turn(("w", 0), w_sb, 0, cp, "s")
         z_turn(0, 0)
         z_turn(0, 1)
-        u_perm(1, 0)
-        quantise(("w", 0), keep, 1, "wq0")
         for jb in range(2, 4):
             m1(0, jb, 1)
             mult(0, jb, 1)
-        quantise(("w", 1), keep, 1, "wq1")
+        quantise(("w", 0), keep, 1, "wq0")
+        u_turn(1, 0)
+        u_turn(1, 1)
         z_quant(0, 0)
         z_quant(0, 1)
-        u_perm(1, 1)
-        u_turn(1, 0)
+        u_perm(1, 2)
+        u_quant(1, 0)
+        u_quant(1, 1)
         z_turn(0, 2)
         z_turn(0, 3)
-        u_quant(1, 0)
-        u_perm(1, 2)
-        u_turn(1, 1)
-        u_turn(1, 2)
-        z_quant(0, 2)
-        z_quant(0, 3)
-        u_quant(1, 1)
+        for cp in range(2):
+            turn(("w", 1), w_sb, 1, cp, "s")
         u_perm(1, 3)
 
-        pending_u = (1, 2)
+        m2_of = {0: (0, 1), 1: (2, 3)}
+        pending = []
         for l in range(1, L):
-            for i in range(4):
+            for i in range(4 if l < L - 1 else 2):
                 pair = [(0, 0), (1, 0)], [(2, 0), (3, 0)], [(0, 1), (1, 1)], [(2, 1), (3, 1)]
                 for jb, h in pair[i]:
                     m1(l, jb, h)
                     mult(l, jb, h)
-                if i == 0:
-                    m2(l - 1, 0)
-                    m2(l - 1, 1)
-                if i == 1:
-                    m2(l - 1, 2)
-                    m2(l - 1, 3)
-                now = (l, 3) if i == 0 else (l + 1, i - 1)
+                for jb in m2_of.get(i if l > 1 else i - 1, ()):
+                    m2(l - 1, jb)
+                now = [(l, 3)] if i == 0 else [(l + 1, i - 1)]
+                if l == 1 and i == 0:
+                    now = [(1, 2), (1, 3)]
                 nxt = (l + 1, i)
-                if pending_u is not None:
-                    u_quant(*pending_u)
-                pending_u = None
-                if now[0] < L:
-                    u_turn(*now)
-                    pending_u = now
-                if i == 0 and l > 1:
+                if l == 1 and i == 0:
+                    quantise(("w", 1), keep, 1, "wq1")
+                for key in pending:
+                    u_quant(*key)
+                pending = []
+                for key in now:
+                    if key[0] < L:
+                        u_turn(*key)
+                        pending.append(key)
+                if i == 0:
                     z_quant(l - 1, 2)
                     z_quant(l - 1, 3)
                 if i == 2:
@@ -264,9 +273,24 @@ def tile_winograd_domain_backward_e3_kernel(tc, g_words, g_scales, u, d, w, out)
                     z_turn(l, 3)
                 if nxt[0] < L:
                     u_perm(*nxt)
-        z_quant(3, 2)
-        m2(3, 0)
-        m2(3, 1)
-        z_quant(3, 3)
-        m2(3, 2)
-        m2(3, 3)
+        l = L - 1
+        m1(l, 0, 1)
+        mult(l, 0, 1)
+        m1(l, 1, 1)
+        mult(l, 1, 1)
+        z_turn(l, 0)
+        m1(l, 2, 1)
+        mult(l, 2, 1)
+        m1(l, 3, 1)
+        z_quant(l, 0)
+        mult(l, 3, 1)
+        z_turn(l, 1)
+        z_turn(l, 2)
+        z_quant(l, 1)
+        m2(l, 0)
+        z_quant(l, 2)
+        z_turn(l, 3, "v")
+        m2(l, 1)
+        z_quant(l, 3)
+        m2(l, 2)
+        m2_split(l, 3)

@@ -43,25 +43,26 @@ def tile_winograd_domain_backward_e3_kernel(tc, g_words, g_scales, u, d, w, out)
             for i in which or range(pieces):
                 nc.sync.dma_start(out=u_sb[l, h][:, n * i : n * i + n, :], in_=rows[:, n * i : n * i + n, :])
 
-        def load_d(l, j0, j1):
+        def load_d(l, j0, j1, h=None):
             rows = d[l].rearrange("(b p) c -> p b c", p=128)
-            nc.sync.dma_start(out=d_sb[l][:, j0:j1, :], in_=rows[:, j0:j1, :])
+            cols = slice(0, 1024) if h is None else slice(512 * h, 512 * h + 512)
+            nc.sync.dma_start(out=d_sb[l][:, j0:j1, cols], in_=rows[:, j0:j1, cols])
 
         def load_g(l0, l1):
             rows = g_words.rearrange("g p n t -> p g (n t)")
             nc.sync.dma_start(out=g_codes[:, :, 512 * l0 : 512 * l1].bitcast(I32),
                               in_=rows[:, :, 2048 * l0 : 2048 * l1].bitcast(I32))
 
-        load_u(0, 0, 2)
+        load_u(0, 0, 4, (0, 1))
+        load_u(0, 0, 2, (1,))
         sc_rows = g_scales.bitcast(I32).rearrange("g (q r) n -> r q g n", r=4)
         for r in range(4):
             nc.scalar.dma_start(out=g_sc[r:128:32, :, :].bitcast(I32), in_=sc_rows[r])
-        load_u(0, 1, 2, (0,))
+        load_u(0, 1, 2)
         load_g(0, 1)
-        load_u(0, 1, 2, (1,))
         load_d(0, 0, 2)
         load_d(0, 2, 4)
-        nc.sync.dma_start(out=w_sb[:], in_=w.rearrange("(b p) c -> p b c", p=128))
+        nc.sync.dma_start(out=w_sb[:], in_=w.rearrange("(p b) c -> p b c", b=4))
         load_u(1, 0, 1)
         load_u(1, 1, 1)
         load_g(1, 2)
@@ -85,12 +86,10 @@ def tile_winograd_domain_backward_e3_kernel(tc, g_words, g_scales, u, d, w, out)
         perm = {}
         quant = {}
 
-        def permute(key, src, g):
-            pt = work.tile([128, 4, 2, 128], F32, name="pt", bufs=3)
-            nc.vector.tensor_copy(
-                out=pt[:],
-                in_=src[:].bitcast(F32)[:, :, 256 * g : 256 * g + 256].rearrange("p c (k u) -> p c u k", u=2),
-            )
+        def permute(key, src, g, engine="v"):
+            pt = work.tile([128, 4, 2, 128], F32, name="pt", bufs=4)
+            copy(engine, pt[:],
+                 src[:].bitcast(F32)[:, :, 256 * g : 256 * g + 256].rearrange("p c (k u) -> p c u k", u=2))
             perm[key] = pt
 
         def turn(key, src, g, cp, engine):
@@ -120,8 +119,8 @@ def tile_winograd_domain_backward_e3_kernel(tc, g_words, g_scales, u, d, w, out)
             for cp in range(2):
                 turn((l, q), u_sb[l, h], g, cp, engines[cp])
 
-        def u_perm(l, q):
-            permute((l, q), u_sb[l, q // 2], q % 2)
+        def u_perm(l, q, engine="v"):
+            permute((l, q), u_sb[l, q // 2], q % 2, engine)
 
         def u_quant(l, q):
             quantise((l, q), work, 8, "uq")
@@ -171,8 +170,8 @@ def tile_winograd_domain_backward_e3_kernel(tc, g_words, g_scales, u, d, w, out)
             zg[l, jb] = zt
 
         def z_quant(l, jb):
-            zc = work.tile([128, 256], U32, name="zc", bufs=6, align_bytes=64)
-            zs = work.tile([128, 256], U8, name="zs", bufs=6, align_bytes=64)
+            zc = work.tile([128, 256], U32, name="zc", bufs=10, align_bytes=64)
+            zs = work.tile([128, 256], U8, name="zs", bufs=10, align_bytes=64)
             nc.vector.quantize_mx(out=zc[:].bitcast(E5), scales=zs[:], in_=zg[l, jb][:])
             zq[l, jb] = (zc, zs)
 
@@ -193,7 +192,7 @@ def tile_winograd_domain_backward_e3_kernel(tc, g_words, g_scales, u, d, w, out)
         def m2(l, jb, engine="s"):
             acc = m2_acc(l, jb)
             ot = work.tile([128, 512], F32, name="ot", bufs=6)
-            copy(engine, ot[:], acc[:])
+            copy(engine, ot[:].rearrange("j (r b) -> j r b", b=4), acc[:].rearrange("j (b r) -> j r b", b=4))
             nc.sync.dma_start(out=out[l, 128 * jb : 128 * jb + 128, :], in_=ot[:])
 
         def m2_split(l, jb):
@@ -201,7 +200,8 @@ def tile_winograd_domain_backward_e3_kernel(tc, g_words, g_scales, u, d, w, out)
             for n, engine in enumerate("sv"):
                 half = slice(256 * n, 256 * n + 256)
                 oh = work.tile([128, 256], F32, name=f"oh{n}", bufs=1)
-                copy(engine, oh[:], acc[:, half])
+                copy(engine, oh[:].rearrange("j (r b) -> j r b", b=4),
+                     acc[:].rearrange("j (b r) -> j r b", b=4)[:, 64 * n : 64 * n + 64, :])
                 nc.sync.dma_start(out=out[l, 128 * jb : 128 * jb + 128, half], in_=oh[:])
 
         for q in (0, 2):
@@ -213,16 +213,15 @@ def tile_winograd_domain_backward_e3_kernel(tc, g_words, g_scales, u, d, w, out)
         for jb in range(4):
             m1(0, jb, 0)
             mult(0, jb, 0)
-        for jb in range(2):
+        for jb in range(3):
             m1(0, jb, 1)
             mult(0, jb, 1)
         for cp in range(2):
             turn(("w", 0), w_sb, 0, cp, "s")
         z_turn(0, 0)
         z_turn(0, 1)
-        for jb in range(2, 4):
-            m1(0, jb, 1)
-            mult(0, jb, 1)
+        m1(0, 3, 1)
+        mult(0, 3, 1)
         quantise(("w", 0), keep, 1, "wq0")
         u_turn(1, 0)
         u_turn(1, 1)
@@ -237,42 +236,80 @@ def tile_winograd_domain_backward_e3_kernel(tc, g_words, g_scales, u, d, w, out)
             turn(("w", 1), w_sb, 1, cp, "s")
         u_perm(1, 3)
 
-        m2_of = {0: (0, 1), 1: (2, 3)}
-        pending = []
-        for l in range(1, L):
-            for i in range(4 if l < L - 1 else 2):
-                pair = [(0, 0), (1, 0)], [(2, 0), (3, 0)], [(0, 1), (1, 1)], [(2, 1), (3, 1)]
-                for jb, h in pair[i]:
-                    m1(l, jb, h)
-                    mult(l, jb, h)
-                for jb in m2_of.get(i if l > 1 else i - 1, ()):
+        for jb in range(2):
+            m1(1, jb, 0)
+            mult(1, jb, 0)
+        quantise(("w", 1), keep, 1, "wq1")
+        u_turn(1, 2)
+        u_turn(1, 3)
+        z_quant(0, 2)
+        z_quant(0, 3)
+        u_perm(2, 0)
+        for jb in range(2, 4):
+            m1(1, jb, 0)
+            mult(1, jb, 0)
+        for jb in range(4):
+            m2(0, jb)
+        u_quant(1, 2)
+        u_perm(2, 1)
+        u_quant(1, 3)
+        u_turn(2, 0)
+        u_turn(2, 1)
+        u_perm(2, 2)
+        u_quant(2, 0)
+        for l in (1, 2, 3):
+            if l > 1:
+                m1(l, 0, 0)
+                mult(l, 0, 0)
+                m1(l, 1, 0)
+                mult(l, 1, 0)
+                m1(l, 2, 0)
+                mult(l, 2, 0)
+                m1(l, 3, 0)
+                mult(l, 3, 0)
+                z_quant(l - 1, 2)
+                z_quant(l - 1, 3)
+                u_quant(l, 2)
+                if l == 2:
+                    u_quant(2, 3)
+                    u_turn(3, 0)
+                else:
+                    u_turn(3, 3)
+                for jb in range(4):
                     m2(l - 1, jb)
-                now = [(l, 3)] if i == 0 else [(l + 1, i - 1)]
-                if l == 1 and i == 0:
-                    now = [(1, 2), (1, 3)]
-                nxt = (l + 1, i)
-                if l == 1 and i == 0:
-                    quantise(("w", 1), keep, 1, "wq1")
-                for key in pending:
-                    u_quant(*key)
-                pending = []
-                for key in now:
-                    if key[0] < L:
-                        u_turn(*key)
-                        pending.append(key)
-                if i == 0:
-                    z_quant(l - 1, 2)
-                    z_quant(l - 1, 3)
-                if i == 2:
-                    z_turn(l, 0)
-                    z_turn(l, 1)
-                if i == 3:
-                    z_turn(l, 2)
-                    z_quant(l, 0)
-                    z_quant(l, 1)
-                    z_turn(l, 3)
-                if nxt[0] < L:
-                    u_perm(*nxt)
+                if l == 2:
+                    u_perm(3, 1)
+                else:
+                    u_quant(3, 3)
+            if l < 3:
+                for jb in range(2):
+                    m1(l, jb, 1)
+                    mult(l, jb, 1)
+                if l == 1:
+                    u_perm(2, 3)
+                    u_quant(2, 1)
+                    u_turn(2, 2)
+                else:
+                    u_quant(3, 0)
+                    u_perm(3, 2)
+                    u_turn(3, 1)
+                z_turn(l, 0)
+                z_turn(l, 1)
+                for jb in range(2, 4):
+                    m1(l, jb, 1)
+                    mult(l, jb, 1)
+                if l == 2:
+                    u_quant(3, 1)
+                    u_turn(3, 2)
+                    u_perm(3, 3)
+                else:
+                    u_turn(2, 3)
+                z_turn(l, 2)
+                z_turn(l, 3)
+                z_quant(l, 0)
+                z_quant(l, 1)
+                if l == 1:
+                    u_perm(3, 0)
         l = L - 1
         m1(l, 0, 1)
         mult(l, 0, 1)

from contextlib import ExitStack

import concourse.mybir as mybir
from concourse.masks import make_identity

F32 = mybir.dt.float32
BF16 = mybir.dt.bfloat16
U32 = mybir.dt.uint32
I32 = mybir.dt.int32
U8 = mybir.dt.uint8
E4 = mybir.dt.float8_e4m3fn_x4
E5 = mybir.dt.float8_e5m2_x4

L, J, O, C, E = 4, 512, 1024, 1024, 512
FLOPS = 2 * L * J * C * (O + E)


def tile_winograd_domain_backward_e3_kernel(tc, g_words, g_scales, u, d, w, out):
    nc = tc.nc
    with ExitStack() as ctx:
        keep = ctx.enter_context(tc.tile_pool(name="keep", bufs=1))
        work = ctx.enter_context(tc.tile_pool(name="work", bufs=2))
        psum = ctx.enter_context(tc.psum_pool(name="psum", bufs=2))
        ctx.enter_context(tc.manual_schedule())

        ident = keep.tile([128, 128], F32, name="ident")
        g_codes = keep.tile([128, 2, 2048], U32, name="g_codes", align_bytes=64)
        g_sc = keep.tile([128, 2, 2048], U8, name="g_sc", align_bytes=64)
        w_sb = keep.tile([128, 4, 1024], BF16, name="w_sb", align_bytes=64)
        u_sb = {}
        d_sb = {}
        for l in range(L):
            for h in range(2):
                u_sb[l, h] = keep.tile([128, 4, 1024], BF16, name=f"u_sb_{l}_{h}", align_bytes=64)
            d_sb[l] = keep.tile([128, 4, 1024], BF16, name=f"d_sb_{l}", align_bytes=64)

        nc.vector.memset(g_sc[:].rearrange("p g n -> p (g n)").bitcast(I32), 0)
        make_identity(nc, ident[:])

        def load_u(l, h, pieces, which=None):
            rows = u[l, 512 * h : 512 * h + 512, :].rearrange("(p c) o -> p c o", c=4)
            n = 4 // pieces
            for i in which or range(pieces):
                nc.sync.dma_start(out=u_sb[l, h][:, n * i : n * i + n, :], in_=rows[:, n * i : n * i + n, :])

        def load_d(l, j0, j1, h=None):
            rows = d[l].rearrange("(b p) c -> p b c", p=128)
            cols = slice(0, 1024) if h is None else slice(512 * h, 512 * h + 512)
            nc.sync.dma_start(out=d_sb[l][:, j0:j1, cols], in_=rows[:, j0:j1, cols])

        def load_g(l0, l1):
            rows = g_words.rearrange("g p n t -> p g (n t)")
            nc.sync.dma_start(out=g_codes[:, :, 512 * l0 : 512 * l1].bitcast(I32),
                              in_=rows[:, :, 2048 * l0 : 2048 * l1].bitcast(I32))

        load_u(0, 0, 4, (0, 1))
        load_u(0, 0, 2, (1,))
        sc_rows = g_scales.bitcast(I32).rearrange("g (q r) n -> r q g n", r=4)
        for r in range(4):
            nc.scalar.dma_start(out=g_sc[r:128:32, :, :].bitcast(I32), in_=sc_rows[r])
        load_u(0, 1, 2)
        load_g(0, 1)
        load_d(0, 0, 2)
        load_d(0, 2, 4)
        nc.sync.dma_start(out=w_sb[:], in_=w.rearrange("(p b) c -> p b c", b=4))
        load_u(1, 0, 1)
        load_u(1, 1, 1)
        load_g(1, 2)
        load_d(1, 0, 2)
        load_d(1, 2, 4)
        load_u(2, 0, 1)
        load_u(2, 1, 1)
        load_g(2, 4)
        load_d(2, 0, 4)
        load_u(3, 0, 1)
        load_u(3, 1, 1)
        load_d(3, 0, 4)

        def copy(engine, dst, src):
            if engine == "s":
                nc.scalar.copy(dst, src)
            else:
                nc.vector.tensor_copy(out=dst, in_=src)

        grouped = {}
        perm = {}
        quant = {}

        def permute(key, src, g, engine="v"):
            pt = work.tile([128, 4, 2, 128], F32, name="pt", bufs=4)
            copy(engine, pt[:],
                 src[:].bitcast(F32)[:, :, 256 * g : 256 * g + 256].rearrange("p c (k u) -> p c u k", u=2))
            perm[key] = pt

        def turn(key, src, g, cp, engine):
            if cp == 0:
                gt = work.tile([128, 2048], BF16, name="gt", bufs=4, align_bytes=64)
                grouped[key] = gt
            xt = psum.tile([128, 2, 2, 128], F32, name="xt", bufs=4)
            for a in range(2):
                for uu in range(2):
                    if key in perm:
                        words = perm[key][:, 2 * cp + a, uu, :]
                    else:
                        words = src[:].bitcast(F32)[:, 2 * cp + a, 256 * g + uu : 256 * g + 256 : 2]
                    nc.tensor.transpose(xt[:, a, uu, :], words, ident[:])
            copy(engine,
                 grouped[key][:].bitcast(F32)[:, 512 * cp : 512 * cp + 512].rearrange("p (a r u) -> p a r u", a=2, u=2),
                 xt[:].rearrange("p a u r -> p a r u"))

        def quantise(key, pool, bufs, tag):
            codes = pool.tile([128, 512], U32, name=tag + "_codes", bufs=bufs, align_bytes=64)
            sc = pool.tile([128, 512], U8, name=tag + "_sc", bufs=bufs, align_bytes=64)
            nc.vector.quantize_mx(out=codes[:].bitcast(E4), scales=sc[:], in_=grouped[key][:])
            quant[key] = (codes, sc)

        def u_turn(l, q, engines="ss"):
            h, g = q // 2, q % 2
            for cp in range(2):
                turn((l, q), u_sb[l, h], g, cp, engines[cp])

        def u_perm(l, q, engine="v"):
            permute((l, q), u_sb[l, q // 2], q % 2, engine)

        def u_quant(l, q):
            quantise((l, q), work, 8, "uq")

        dz = {}
        acc1 = {}

        def m1(l, jb, h):
            acc = psum.tile([128, 512], F32, name="acc", bufs=4)
            cols = slice(512 * l + 128 * jb, 512 * l + 128 * jb + 128)
            for g in range(2):
                codes, sc = quant[l, 2 * h + g]
                nc.tensor.matmul_mx(
                    out=acc[:],
                    lhsT=g_codes[:, g, cols].bitcast(E5), lhsT_scale=g_sc[:, g, cols],
                    rhs=codes[:].bitcast(E4), rhs_scale=sc[:],
                    start=(g == 0), stop=(g == 1),
                )
            acc1[l, jb, h] = acc

        def mult(l, jb, h):
            if h == 0:
                z = work.tile([128, 1024], BF16, name="z", bufs=6, align_bytes=64)
                dz[l, jb] = z
            half = slice(512 * h, 512 * h + 512)
            nc.vector.tensor_tensor(
                out=dz[l, jb][:, half].rearrange("j (u p e) -> j u p e", u=2, e=2),
                in0=acc1[l, jb, h][:].rearrange("j (u e p) -> j u p e", u=2, e=2),
                in1=d_sb[l][:, jb, half].rearrange("j (p u e) -> j u p e", u=2, e=2),
                op=mybir.AluOpType.mult,
            )

        zg = {}
        zq = {}

        def z_turn(l, jb, engine="s"):
            zt = work.tile([128, 1024], BF16, name="zt", bufs=4, align_bytes=64)
            xt = psum.tile([128, 2, 2, 128], F32, name="xt", bufs=4)
            words = dz[l, jb][:].bitcast(F32)
            for h in range(2):
                for uu in range(2):
                    c0 = 256 * h + 128 * uu
                    nc.tensor.transpose(xt[:, h, uu, :], words[:, c0 : c0 + 128], ident[:])
            copy(engine,
                 zt[:].bitcast(F32).rearrange("p (h j u) -> p h j u", h=2, u=2),
                 xt[:].rearrange("p h u j -> p h j u"))
            zg[l, jb] = zt

        def z_quant(l, jb):
            zc = work.tile([128, 256], U32, name="zc", bufs=10, align_bytes=64)
            zs = work.tile([128, 256], U8, name="zs", bufs=10, align_bytes=64)
            nc.vector.quantize_mx(out=zc[:].bitcast(E5), scales=zs[:], in_=zg[l, jb][:])
            zq[l, jb] = (zc, zs)

        def m2_acc(l, jb):
            acc = psum.tile([128, 512], F32, name="acc", bufs=4)
            zc, zs = zq[l, jb]
            for h in range(2):
                codes, sc = quant["w", h]
                cols = slice(128 * h, 128 * h + 128)
                nc.tensor.matmul_mx(
                    out=acc[:],
                    lhsT=zc[:, cols].bitcast(E5), lhsT_scale=zs[:, cols],
                    rhs=codes[:].bitcast(E4), rhs_scale=sc[:],
                    start=(h == 0), stop=(h == 1),
                )
            return acc

        def m2(l, jb, engine="s"):
            acc = m2_acc(l, jb)
            ot = work.tile([128, 512], F32, name="ot", bufs=6)
            copy(engine, ot[:].rearrange("j (r b) -> j r b", b=4), acc[:].rearrange("j (b r) -> j r b", b=4))
            nc.sync.dma_start(out=out[l, 128 * jb : 128 * jb + 128, :], in_=ot[:])

        def m2_split(l, jb):
            acc = m2_acc(l, jb)
            for n, engine in enumerate("sv"):
                half = slice(256 * n, 256 * n + 256)
                oh = work.tile([128, 256], F32, name=f"oh{n}", bufs=1)
                copy(engine, oh[:].rearrange("j (r b) -> j r b", b=4),
                     acc[:].rearrange("j (b r) -> j r b", b=4)[:, 64 * n : 64 * n + 64, :])
                nc.sync.dma_start(out=out[l, 128 * jb : 128 * jb + 128, half], in_=oh[:])

        for q in (0, 2):
            for cp in range(2):
                turn((0, q), u_sb[0, q // 2], 0, cp, "s")
                turn((0, q + 1), u_sb[0, q // 2], 1, cp, "v" if cp == 0 or q == 0 else "s")
            u_quant(0, q)
            u_quant(0, q + 1)
        for jb in range(4):
            m1(0, jb, 0)
            mult(0, jb, 0)
        for jb in range(3):
            m1(0, jb, 1)
            mult(0, jb, 1)
        for cp in range(2):
            turn(("w", 0), w_sb, 0, cp, "s")
        z_turn(0, 0)
        z_turn(0, 1)
        m1(0, 3, 1)
        mult(0, 3, 1)
        quantise(("w", 0), keep, 1, "wq0")
        u_turn(1, 0)
        u_turn(1, 1)
        z_quant(0, 0)
        z_quant(0, 1)
        u_perm(1, 2)
        u_quant(1, 0)
        u_quant(1, 1)
        z_turn(0, 2)
        z_turn(0, 3)
        for cp in range(2):
            turn(("w", 1), w_sb, 1, cp, "s")
        u_perm(1, 3)

        for jb in range(2):
            m1(1, jb, 0)
            mult(1, jb, 0)
        quantise(("w", 1), keep, 1, "wq1")
        u_turn(1, 2)
        u_turn(1, 3)
        z_quant(0, 2)
        z_quant(0, 3)
        u_perm(2, 0)
        for jb in range(2, 4):
            m1(1, jb, 0)
            mult(1, jb, 0)
        for jb in range(4):
            m2(0, jb)
        u_quant(1, 2)
        u_perm(2, 1)
        u_quant(1, 3)
        u_turn(2, 0)
        u_turn(2, 1)
        u_perm(2, 2)
        u_quant(2, 0)
        for l in (1, 2, 3):
            if l > 1:
                m1(l, 0, 0)
                mult(l, 0, 0)
                m1(l, 1, 0)
                mult(l, 1, 0)
                m1(l, 2, 0)
                mult(l, 2, 0)
                m1(l, 3, 0)
                mult(l, 3, 0)
                z_quant(l - 1, 2)
                z_quant(l - 1, 3)
                u_quant(l, 2)
                if l == 2:
                    u_quant(2, 3)
                    u_turn(3, 0)
                else:
                    u_turn(3, 3)
                for jb in range(4):
                    m2(l - 1, jb)
                if l == 2:
                    u_perm(3, 1)
                else:
                    u_quant(3, 3)
            if l < 3:
                for jb in range(2):
                    m1(l, jb, 1)
                    mult(l, jb, 1)
                if l == 1:
                    u_perm(2, 3)
                    u_quant(2, 1)
                    u_turn(2, 2)
                else:
                    u_quant(3, 0)
                    u_perm(3, 2)
                    u_turn(3, 1)
                z_turn(l, 0)
                z_turn(l, 1)
                for jb in range(2, 4):
                    m1(l, jb, 1)
                    mult(l, jb, 1)
                if l == 2:
                    u_quant(3, 1)
                    u_turn(3, 2)
                    u_perm(3, 3)
                else:
                    u_turn(2, 3)
                z_turn(l, 2)
                z_turn(l, 3)
                z_quant(l, 0)
                z_quant(l, 1)
                if l == 1:
                    u_perm(3, 0)
        l = L - 1
        m1(l, 0, 1)
        mult(l, 0, 1)
        m1(l, 1, 1)
        mult(l, 1, 1)
        z_turn(l, 0)
        m1(l, 2, 1)
        mult(l, 2, 1)
        m1(l, 3, 1)
        z_quant(l, 0)
        mult(l, 3, 1)
        z_turn(l, 1)
        z_turn(l, 2)
        z_quant(l, 1)
        m2(l, 0)
        z_quant(l, 2)
        z_turn(l, 3, "v")
        m2(l, 1)
        z_quant(l, 3)
        m2(l, 2)
        m2_split(l, 3)
